import numpy as np, ml_dtypes
CORES = [211,219,227,235,243,251,83,91,99,107,115,123]
N = 12
import mx_ref
NC, G = 128, 4
C = np.float32(0.037)
BF = ml_dtypes.bfloat16
def cut(t, i, w=512):
    return t[:, w * i:w * i + w]
def tile(rs):
    return np.stack(rs, axis=2).reshape(128, -1).astype(BF)
def layer(w, X):
    out = []
    for i in range(G):
        for t in range(len(X)):
            p = mx_ref.matmul(mx_ref.quantize(cut(w, len(X) * i + t)), X[t])
            z = p if t == 0 else z + p
        out.append(z)
    return out
def act(Z):
    return [np.maximum(z, 0) * C for z in Z]
def setup_inputs(rng):
    def f(*shape):
        return mx_ref.flush((rng.standard_normal(shape, dtype=np.float32) * np.exp2(rng.integers(-2, 3, shape[:-1] + (1,)))).astype(BF))
    return {"xk": f(N, 128, 512), "xq": f(N, 128, 4 * NC), "wk": f(N, 128, G * 512), "wq": f(N, 128, G * 512)}
def setup_inputs_blocks(rng):
    d = setup_inputs(rng)
    for k in ("xk", "xq", "wk", "wq"): d[k] = mx_ref.spread(d[k], rng, 4)
    return d
def setup_inputs_wide(rng):
    d = setup_inputs(rng)
    for k in ("xk", "xq", "wk", "wq"): d[k] = mx_ref.flush((d[k].astype(np.float32) * np.exp2(rng.integers(-5, 6, (N, 1, 1))).astype(np.float32)).astype(BF))
    return d
def reference(xk, xq, wk, wq):
    K = [mx_ref.quantize(tile(act(layer(wk[j], [mx_ref.quantize(xk[j])])))) for j in range(N)]
    y = np.zeros((N, 128, N * NC), np.float32)
    for r in range(N):
        q = mx_ref.quantize(tile(act(layer(wq[r], [mx_ref.quantize(xq[r])]))))
        for j in range(N):
            y[r][:, NC * j:NC * j + NC] = mx_ref.matmul(K[j], q)
    return {"y": y}

@@ -1,0 +1,212 @@
+from concourse.bass import DstId, RemoteDMATransfer
+from concourse.mybir import dt, ActivationFunctionType
+
+N = 12
+NC = 128
+G = 4
+C = 0.037
+WORLD = 256
+BANK = 512
+NBANKS = 8
+
+X4 = "float8_e4m3fn_x4"
+SCRATCH = {
+    "xk_t": ("sbuf", [128, 4 * NC], "bfloat16"), "wk_t": ("sbuf", [128, G * 512], "bfloat16"),
+    "xq_t": ("sbuf", [128, 4 * NC], "bfloat16"), "wq_t": ("sbuf", [128, G * 512], "bfloat16"),
+    "xk_c": ("sbuf", [128, NC], X4), "xk_s": ("sbuf", [128, NC], "uint8"),
+    "xq_c": ("sbuf", [128, NC], X4), "xq_s": ("sbuf", [128, NC], "uint8"),
+    "wk_c": ("sbuf", [128, G * 128], X4), "wk_s": ("sbuf", [128, G * 128], "uint8"),
+    "wq_c": ("sbuf", [128, G * 128], X4), "wq_s": ("sbuf", [128, G * 128], "uint8"),
+    "k_t": ("sbuf", [128, 512], "bfloat16"), "q_t": ("sbuf", [128, 4 * NC], "bfloat16"),
+    "kc": ("sbuf", [128, N * 128], X4), "ks": ("sbuf", [128, N * 128], "uint8"),
+    "q_c": ("sbuf", [128, NC], X4), "q_s": ("sbuf", [128, NC], "uint8"),
+    "ps": ("psum", [128, NBANKS * BANK], "float32"),
+    "yb": ("sbuf", [128, N * NC], "float32"),
+}
+SEMAPHORES = (
+    ["l_xk", "l_wk", "l_xq", "l_wq", "q_xk", "q_xq", "a_k", "a_q", "q_k", "q_q", "st", "sent"]
+    + ["q_wk%d" % i for i in range(G)] + ["q_wq%d" % i for i in range(G)]
+    + ["m_k%d" % i for i in range(G)] + ["m_q%d" % i for i in range(G)]
+    + ["c%d" % j for j in range(N)] + ["s%d" % j for j in range(N)]
+    + ["m_y%d" % t for t in range(N)] + ["cp%d" % t for t in range(N)]
+)
+
+DIRECT_PAIRS = 2
+DIRECT_SLOTS = [0, 1, 3]
+HELPER_SLOTS = [2, 4, 5]
+
+_CACHE = {}
+
+
+def _bits(mask):
+    return [b for b in range(16) if (mask >> b) & 1]
+
+
+def _mask(bits):
+    return sum(1 << b for b in bits)
+
+
+def _plan(T, topo, j):
+    if j in _CACHE:
+        return _CACHE[j]
+    cores = list(T.cores)
+    R = cores[j]
+    others = sorted((i for i in range(N) if i != j), key=lambda i: (i - j) % N)
+    mate = [i for i in others if topo.mates(R, cores[i])]
+    same = [i for i in others if topo.same_plane(R, cores[i])]
+    pairs = [[s] + [i for i in others if topo.mates(cores[s], cores[i])] for s in same]
+    chip = [c for c in range(WORLD) if topo.host(c) == topo.host(R) and topo.chip(c) == topo.chip(R)]
+    helpers = [c for c in chip if c != R and all(topo.may_write(c, cores[i]) for i in others)]
+    helpers.sort(key=lambda c: (topo.die(c) == topo.die(R), c))
+    parcels = [(R, mate, DIRECT_SLOTS[0])]
+    for d in range(DIRECT_PAIRS):
+        parcels.append((R, pairs[d], DIRECT_SLOTS[1 + d]))
+    for h, p in enumerate(pairs[DIRECT_PAIRS:]):
+        parcels.append((helpers[h], p, HELPER_SLOTS[h]))
+    _CACHE[j] = parcels
+    return parcels
+
+
+def _codes(T, j):
+    return T.kc[:, 128 * j:128 * j + 128].bitcast(dt.uint8)
+
+
+def _plane(T, j):
+    return T.ks[:, 128 * j:128 * j + 128]
+
+
+def _send(g, T, topo, core, j, dst_cores, mask):
+    ids = []
+    for d in dst_cores:
+        rid, pid = topo.addr(d, core)
+        ids.append(DstId(rid=rid, pnc=pid))
+    n = len(dst_cores)
+    return [
+        lambda: g.remote_dma_fused([RemoteDMATransfer(dst_ids=ids, dma_engine_mask=mask, remote_sem=T.sem["c%d" % j],
+                                                      srcs=[_codes(T, j)], dsts=[_codes(T, j)] * n)], local_sem=T.sem.sent),
+        lambda: g.remote_dma_fused([RemoteDMATransfer(dst_ids=ids, dma_engine_mask=mask, remote_sem=T.sem["s%d" % j],
+                                                      srcs=[_plane(T, j)], dsts=[_plane(T, j)] * n)], local_sem=T.sem.sent),
+    ]
+
+
+def _masks(T, topo, j):
+    cores = list(T.cores)
+    R = cores[j]
+    parcels = _plan(T, topo, j)
+    off = topo.mask(R, cores[parcels[0][1][0]])
+    hs = [p[0] for p in parcels if p[0] != R]
+    on = topo.mask(R, hs[0]) if hs else 0
+    return _mask([b for b in _bits(on) if b not in _bits(off)]), off
+
+
+def _helper(g, core, T, topo, j, dsts):
+    cores = list(T.cores)
+    on, _ = _masks(T, topo, j)
+    m = topo.mask(core, cores[dsts[0]])
+    codes, plane = _send(g, T, topo, core, j, [cores[d] for d in dsts], m)
+    g.wait_ge(T.sem["c%d" % j], len(_bits(on)))
+    codes()
+    g.wait_ge(T.sem["s%d" % j], len(_bits(on)))
+    plane()
+    g.wait_ge(T.sem.sent, 2 * len(_bits(m)))
+
+
+def _tile(g, T, x_t, w_t, x_c, x_s, w_c, w_s, tile, out_c, out_s, tag, bank0):
+    S = T.sem
+    v, t, a = g.vector, g.tensor, g.scalar
+    v.wait_ge(S["l_x" + tag], 16)
+    v.quantize_mx(x_c[:], x_s[:], x_t[:]).then_inc(S["q_x" + tag], 1)
+    v.wait_ge(S["l_w" + tag], 16)
+    t.wait_ge(S["q_x" + tag], 1)
+    for i in range(G):
+        v.quantize_mx(w_c[:, 128 * i:128 * i + 128], w_s[:, 128 * i:128 * i + 128],
+                      w_t[:, 512 * i:512 * i + 512]).then_inc(S["q_w%s%d" % (tag, i)], 1)
+        z = T.ps[:, BANK * (bank0 + i):BANK * (bank0 + i) + NC]
+        t.wait_ge(S["q_w%s%d" % (tag, i)], 1)
+        t.matmul_mx(z, w_c[:, 128 * i:128 * i + 128], w_s[:, 128 * i:128 * i + 128], x_c[:], x_s[:],
+                    True, True).then_inc(S["m_%s%d" % (tag, i)], 1)
+        a.wait_ge(S["m_%s%d" % (tag, i)], 1)
+        a.activation(tile[:, i:4 * NC:4], z, ActivationFunctionType.Relu, scale=C).then_inc(S["a_" + tag], 1)
+    v.wait_ge(S["a_" + tag], G)
+    v.quantize_mx(out_c, out_s, tile[:]).then_inc(S["q_" + tag], 1)
+
+
+def rank_program(g, core, T, topo):
+    cores = list(T.cores)
+    r = T.rank_of(core)
+    if r is None:
+        for j in range(N):
+            for snd, dsts, _ in _plan(T, topo, j):
+                if snd == core:
+                    _helper(g, core, T, topo, j, dsts)
+        return
+    S = T.sem
+
+    g.sync.dma_start(T.xk_t[:], T.xk[:]).then_inc(S.l_xk, 16)
+    g.scalar.dma_start(T.wk_t[:], T.wk[:]).then_inc(S.l_wk, 16)
+    g.sync.dma_start(T.xq_t[:], T.xq[:]).then_inc(S.l_xq, 16)
+    g.scalar.dma_start(T.wq_t[:], T.wq[:]).then_inc(S.l_wq, 16)
+
+    _tile(g, T, T.xk_t, T.wk_t, T.xk_c, T.xk_s, T.wk_c, T.wk_s, T.k_t,
+          T.kc[:, 128 * r:128 * r + 128], T.ks[:, 128 * r:128 * r + 128], "k", 0)
+    _tile(g, T, T.xq_t, T.wq_t, T.xq_c, T.xq_s, T.wq_c, T.wq_s, T.q_t, T.q_c[:], T.q_s[:], "q", G)
+
+    parcels = _plan(T, topo, r)
+    on, off = _masks(T, topo, r)
+    hs = [p[0] for p in parcels if p[0] != core]
+    direct = [cores[d] for p in sorted((p for p in parcels if p[0] == core), key=lambda p: p[2]) for d in p[1]]
+    g.wait_ge(S.q_k, 1)
+    sent = 0
+    for dst, m in ((hs, on), (direct, off)):
+        if dst:
+            for call in _send(g, T, topo, core, r, dst, m):
+                call()
+                sent += len(_bits(m))
+
+    where = {}
+    for j in range(N):
+        if j == r:
+            continue
+        for snd, dsts, slot in _plan(T, topo, j):
+            if r in dsts:
+                where[j] = (slot, dsts.index(r), len(_bits(topo.mask(snd, core))))
+    seq = [r] + sorted(where, key=lambda j: where[j][:2])
+    groups = {}
+    for j in seq:
+        groups.setdefault(where[j][0] if j != r else DIRECT_SLOTS[0], []).append(j)
+    t = g.tensor
+    t.wait_ge(S.q_k, 1)
+    t.wait_ge(S.q_q, 1)
+    for n, j in enumerate(seq):
+        if j != r:
+            t.wait_ge(S["c%d" % j], where[j][2])
+            t.wait_ge(S["s%d" % j], where[j][2])
+        if n >= NBANKS:
+            t.wait_ge(S["cp%d" % (n - NBANKS)], 1)
+        z = T.ps[:, BANK * (n % NBANKS):BANK * (n % NBANKS) + NC]
+        t.matmul_mx(z, T.kc[:, 128 * j:128 * j + 128], T.ks[:, 128 * j:128 * j + 128], T.q_c[:], T.q_s[:],
+                    True, True).then_inc(S["m_y%d" % n], 1)
+        out = T.yb[:, NC * j:NC * j + NC]
+        if n % 2 == 0:
+            g.scalar.wait_ge(S["m_y%d" % n], 1)
+            g.scalar.activation(out, z, ActivationFunctionType.Copy).then_inc(S["cp%d" % n], 1)
+        else:
+            g.vector.wait_ge(S["m_y%d" % n], 1)
+            g.vector.tensor_copy(out, z).then_inc(S["cp%d" % n], 1)
+
+    stores = 0
+    for slot in sorted(groups):
+        js = sorted(groups[slot])
+        for j in js:
+            g.sync.wait_ge(S["cp%d" % seq.index(j)], 1)
+        runs = []
+        for j in js:
+            if runs and runs[-1][1] == j:
+                runs[-1][1] = j + 1
+            else:
+                runs.append([j, j + 1])
+        for a, b in runs:
+            g.sync.dma_start(T.y[:, NC * a:NC * b], T.yb[:, NC * a:NC * b]).then_inc(S.st, 16)
+            stores += 1
+    g.sync.wait_ge(S.st, 16 * stores)
+    g.wait_ge(S.sent, sent)

@@ -24,16 +24,15 @@ SCRATCH = {
     "yb": ("sbuf", [128, N * NC], "float32"),
 }
 SEMAPHORES = (
-    ["l_xk", "l_wk", "l_xq", "l_wq", "q_xk", "q_xq", "a_k", "a_q", "q_k", "q_q", "st", "sent"]
+    ["l_xk", "l_wk0", "l_wk1", "l_xq", "l_wq0", "q_xk", "q_xq", "a_k", "a_q", "q_k", "q_q", "st", "sent"]
     + ["q_wk%d" % i for i in range(G)] + ["q_wq%d" % i for i in range(G)]
     + ["m_k%d" % i for i in range(G)] + ["m_q%d" % i for i in range(G)]
     + ["c%d" % j for j in range(N)] + ["s%d" % j for j in range(N)]
     + ["m_y%d" % t for t in range(N)] + ["cp%d" % t for t in range(N)]
 )
 
-DIRECT_PAIRS = 2
-DIRECT_SLOTS = [0, 1, 3]
-HELPER_SLOTS = [2, 4, 5]
+SPLIT_PAIRS = 2
+WK_LOADS = [(0, 3), (3, 4)]
 
 _CACHE = {}
 
@@ -55,14 +54,16 @@ def _plan(T, topo, j):
     mate = [i for i in others if topo.mates(R, cores[i])]
     same = [i for i in others if topo.same_plane(R, cores[i])]
     pairs = [[s] + [i for i in others if topo.mates(cores[s], cores[i])] for s in same]
-    chip = [c for c in range(WORLD) if topo.host(c) == topo.host(R) and topo.chip(c) == topo.chip(R)]
-    helpers = [c for c in chip if c != R and all(topo.may_write(c, cores[i]) for i in others)]
-    helpers.sort(key=lambda c: (topo.die(c) == topo.die(R), c))
-    parcels = [(R, mate, DIRECT_SLOTS[0])]
-    for d in range(DIRECT_PAIRS):
-        parcels.append((R, pairs[d], DIRECT_SLOTS[1 + d]))
-    for h, p in enumerate(pairs[DIRECT_PAIRS:]):
-        parcels.append((helpers[h], p, HELPER_SLOTS[h]))
+    chip = [c for c in range(WORLD) if c != R and topo.host(c) == topo.host(R) and topo.chip(c) == topo.chip(R)]
+    ports = [c for c in chip if all(topo.may_write(c, cores[i]) for i in others)]
+    ports.sort(key=lambda c: (topo.die(c) == topo.die(R), c))
+    plain = [c for c in chip if c not in ports and all(topo.may_write(c, cores[i]) for i in same)]
+    plain.sort(key=lambda c: (topo.die(c) != topo.die(R), c))
+    near, far = pairs[:SPLIT_PAIRS], pairs[SPLIT_PAIRS:]
+    parcels = [(R, mate + [p[1] for p in near])]
+    for h, p in enumerate(far):
+        parcels.append((ports[h], p))
+    parcels.append((plain[0], [p[0] for p in near]))
     _CACHE[j] = parcels
     return parcels
 
@@ -75,18 +76,14 @@ def _plane(T, j):
     return T.ks[:, 128 * j:128 * j + 128]
 
 
-def _send(g, T, topo, core, j, dst_cores, mask):
+def _transfer(T, topo, core, j, dst_cores, mask, codes):
     ids = []
     for d in dst_cores:
         rid, pid = topo.addr(d, core)
         ids.append(DstId(rid=rid, pnc=pid))
-    n = len(dst_cores)
-    return [
-        lambda: g.remote_dma_fused([RemoteDMATransfer(dst_ids=ids, dma_engine_mask=mask, remote_sem=T.sem["c%d" % j],
-                                                      srcs=[_codes(T, j)], dsts=[_codes(T, j)] * n)], local_sem=T.sem.sent),
-        lambda: g.remote_dma_fused([RemoteDMATransfer(dst_ids=ids, dma_engine_mask=mask, remote_sem=T.sem["s%d" % j],
-                                                      srcs=[_plane(T, j)], dsts=[_plane(T, j)] * n)], local_sem=T.sem.sent),
-    ]
+    ap = _codes(T, j) if codes else _plane(T, j)
+    return RemoteDMATransfer(dst_ids=ids, dma_engine_mask=mask, remote_sem=T.sem[("c%d" if codes else "s%d") % j],
+                             srcs=[ap], dsts=[ap] * len(dst_cores))
 
 
 def _masks(T, topo, j):
@@ -103,30 +100,31 @@ def _helper(g, core, T, topo, j, dsts):
     cores = list(T.cores)
     on, _ = _masks(T, topo, j)
     m = topo.mask(core, cores[dsts[0]])
-    codes, plane = _send(g, T, topo, core, j, [cores[d] for d in dsts], m)
-    g.wait_ge(T.sem["c%d" % j], len(_bits(on)))
-    codes()
     g.wait_ge(T.sem["s%d" % j], len(_bits(on)))
-    plane()
-    g.wait_ge(T.sem.sent, 2 * len(_bits(m)))
+    g.remote_dma_fused([_transfer(T, topo, core, j, [cores[d] for d in dsts], m, False)], local_sem=T.sem.sent)
+    g.wait_ge(T.sem["c%d" % j], len(_bits(on)))
+    for d in dsts:
+        g.remote_dma_fused([_transfer(T, topo, core, j, [cores[d]], m, True)], local_sem=T.sem.sent)
+    g.wait_ge(T.sem.sent, (1 + len(dsts)) * len(_bits(m)))
 
 
-def _tile(g, T, x_t, w_t, x_c, x_s, w_c, w_s, tile, out_c, out_s, tag, bank0):
+def _tile(g, T, x_t, w_t, x_c, x_s, w_c, w_s, tile, out_c, out_s, tag, bank0, loads):
     S = T.sem
     v, t, a = g.vector, g.tensor, g.scalar
     v.wait_ge(S["l_x" + tag], 16)
     v.quantize_mx(x_c[:], x_s[:], x_t[:]).then_inc(S["q_x" + tag], 1)
-    v.wait_ge(S["l_w" + tag], 16)
     t.wait_ge(S["q_x" + tag], 1)
-    for i in range(G):
-        v.quantize_mx(w_c[:, 128 * i:128 * i + 128], w_s[:, 128 * i:128 * i + 128],
-                      w_t[:, 512 * i:512 * i + 512]).then_inc(S["q_w%s%d" % (tag, i)], 1)
-        z = T.ps[:, BANK * (bank0 + i):BANK * (bank0 + i) + NC]
-        t.wait_ge(S["q_w%s%d" % (tag, i)], 1)
-        t.matmul_mx(z, w_c[:, 128 * i:128 * i + 128], w_s[:, 128 * i:128 * i + 128], x_c[:], x_s[:],
-                    True, True).then_inc(S["m_%s%d" % (tag, i)], 1)
-        a.wait_ge(S["m_%s%d" % (tag, i)], 1)
-        a.activation(tile[:, i:4 * NC:4], z, ActivationFunctionType.Relu, scale=C).then_inc(S["a_" + tag], 1)
+    for n, (lo, hi) in enumerate(loads):
+        v.wait_ge(S["l_w%s%d" % (tag, n)], 16)
+        for i in range(lo, hi):
+            v.quantize_mx(w_c[:, 128 * i:128 * i + 128], w_s[:, 128 * i:128 * i + 128],
+                          w_t[:, 512 * i:512 * i + 512]).then_inc(S["q_w%s%d" % (tag, i)], 1)
+            z = T.ps[:, BANK * (bank0 + i):BANK * (bank0 + i) + NC]
+            t.wait_ge(S["q_w%s%d" % (tag, i)], 1)
+            t.matmul_mx(z, w_c[:, 128 * i:128 * i + 128], w_s[:, 128 * i:128 * i + 128], x_c[:], x_s[:],
+                        True, True).then_inc(S["m_%s%d" % (tag, i)], 1)
+            a.wait_ge(S["m_%s%d" % (tag, i)], 1)
+            a.activation(tile[:, i:4 * NC:4], z, ActivationFunctionType.Relu, scale=C).then_inc(S["a_" + tag], 1)
     v.wait_ge(S["a_" + tag], G)
     v.quantize_mx(out_c, out_s, tile[:]).then_inc(S["q_" + tag], 1)
 
@@ -136,51 +134,50 @@ def rank_program(g, core, T, topo):
     r = T.rank_of(core)
     if r is None:
         for j in range(N):
-            for snd, dsts, _ in _plan(T, topo, j):
+            for snd, dsts in _plan(T, topo, j):
                 if snd == core:
                     _helper(g, core, T, topo, j, dsts)
         return
     S = T.sem
 
+    (a0, b0), (a1, b1) = WK_LOADS
     g.sync.dma_start(T.xk_t[:], T.xk[:]).then_inc(S.l_xk, 16)
-    g.scalar.dma_start(T.wk_t[:], T.wk[:]).then_inc(S.l_wk, 16)
+    g.scalar.dma_start(T.wk_t[:, 512 * a0:512 * b0], T.wk[:, 512 * a0:512 * b0]).then_inc(S.l_wk0, 16)
+    g.sync.dma_start(T.wk_t[:, 512 * a1:512 * b1], T.wk[:, 512 * a1:512 * b1]).then_inc(S.l_wk1, 16)
     g.sync.dma_start(T.xq_t[:], T.xq[:]).then_inc(S.l_xq, 16)
-    g.scalar.dma_start(T.wq_t[:], T.wq[:]).then_inc(S.l_wq, 16)
+    g.scalar.dma_start(T.wq_t[:], T.wq[:]).then_inc(S.l_wq0, 16)
 
     _tile(g, T, T.xk_t, T.wk_t, T.xk_c, T.xk_s, T.wk_c, T.wk_s, T.k_t,
-          T.kc[:, 128 * r:128 * r + 128], T.ks[:, 128 * r:128 * r + 128], "k", 0)
-    _tile(g, T, T.xq_t, T.wq_t, T.xq_c, T.xq_s, T.wq_c, T.wq_s, T.q_t, T.q_c[:], T.q_s[:], "q", G)
+          T.kc[:, 128 * r:128 * r + 128], T.ks[:, 128 * r:128 * r + 128], "k", 0, WK_LOADS)
+    _tile(g, T, T.xq_t, T.wq_t, T.xq_c, T.xq_s, T.wq_c, T.wq_s, T.q_t, T.q_c[:], T.q_s[:], "q", G, [(0, G)])
 
     parcels = _plan(T, topo, r)
     on, off = _masks(T, topo, r)
     hs = [p[0] for p in parcels if p[0] != core]
-    direct = [cores[d] for p in sorted((p for p in parcels if p[0] == core), key=lambda p: p[2]) for d in p[1]]
+    own = [cores[d] for p in parcels if p[0] == core for d in p[1]]
     g.wait_ge(S.q_k, 1)
-    sent = 0
-    for dst, m in ((hs, on), (direct, off)):
-        if dst:
-            for call in _send(g, T, topo, core, r, dst, m):
-                call()
-                sent += len(_bits(m))
+    for dst, m in ((hs, on), (own, off)):
+        g.remote_dma_fused([_transfer(T, topo, core, r, dst, m, False)], local_sem=S.sent)
+        g.remote_dma_fused([_transfer(T, topo, core, r, dst, m, True)], local_sem=S.sent)
+    sent = 2 * len(_bits(on)) + 2 * len(_bits(off))
 
-    where = {}
+    when, unit, count = {r: (0, 0)}, {r: (0, 0)}, {}
     for j in range(N):
         if j == r:
             continue
-        for snd, dsts, slot in _plan(T, topo, j):
+        for p, (snd, dsts) in enumerate(_plan(T, topo, j)):
             if r in dsts:
-                where[j] = (slot, dsts.index(r), len(_bits(topo.mask(snd, core))))
-    seq = [r] + sorted(where, key=lambda j: where[j][:2])
-    groups = {}
-    for j in seq:
-        groups.setdefault(where[j][0] if j != r else DIRECT_SLOTS[0], []).append(j)
+                count[j] = len(_bits(topo.mask(snd, core)))
+                when[j] = (1, dsts.index(r)) if snd == cores[j] else (2 + dsts.index(r), p)
+                unit[j] = (0, 0) if topo.mates(cores[j], core) else (1, j)
+    seq = sorted(when, key=lambda j: when[j])
     t = g.tensor
     t.wait_ge(S.q_k, 1)
     t.wait_ge(S.q_q, 1)
     for n, j in enumerate(seq):
         if j != r:
-            t.wait_ge(S["c%d" % j], where[j][2])
-            t.wait_ge(S["s%d" % j], where[j][2])
+            t.wait_ge(S["s%d" % j], count[j])
+            t.wait_ge(S["c%d" % j], count[j])
         if n >= NBANKS:
             t.wait_ge(S["cp%d" % (n - NBANKS)], 1)
         z = T.ps[:, BANK * (n % NBANKS):BANK * (n % NBANKS) + NC]
@@ -194,9 +191,12 @@ def rank_program(g, core, T, topo):
             g.vector.wait_ge(S["m_y%d" % n], 1)
             g.vector.tensor_copy(out, z).then_inc(S["cp%d" % n], 1)
 
+    units = {}
+    for j in seq:
+        units.setdefault(unit[j], []).append(j)
     stores = 0
-    for slot in sorted(groups):
-        js = sorted(groups[slot])
+    for js in sorted(units.values(), key=lambda js: max(seq.index(j) for j in js)):
+        js = sorted(js)
         for j in js:
             g.sync.wait_ge(S["cp%d" % seq.index(j)], 1)
         runs = []

from concourse.bass import DstId, RemoteDMATransfer
from concourse.mybir import dt, ActivationFunctionType

N = 12
NC = 128
G = 4
C = 0.037
WORLD = 256
BANK = 512
NBANKS = 8

X4 = "float8_e4m3fn_x4"
SCRATCH = {
    "xk_t": ("sbuf", [128, 4 * NC], "bfloat16"), "wk_t": ("sbuf", [128, G * 512], "bfloat16"),
    "xq_t": ("sbuf", [128, 4 * NC], "bfloat16"), "wq_t": ("sbuf", [128, G * 512], "bfloat16"),
    "xk_c": ("sbuf", [128, NC], X4), "xk_s": ("sbuf", [128, NC], "uint8"),
    "xq_c": ("sbuf", [128, NC], X4), "xq_s": ("sbuf", [128, NC], "uint8"),
    "wk_c": ("sbuf", [128, G * 128], X4), "wk_s": ("sbuf", [128, G * 128], "uint8"),
    "wq_c": ("sbuf", [128, G * 128], X4), "wq_s": ("sbuf", [128, G * 128], "uint8"),
    "k_t": ("sbuf", [128, 512], "bfloat16"), "q_t": ("sbuf", [128, 4 * NC], "bfloat16"),
    "kc": ("sbuf", [128, N * 128], X4), "ks": ("sbuf", [128, N * 128], "uint8"),
    "q_c": ("sbuf", [128, NC], X4), "q_s": ("sbuf", [128, NC], "uint8"),
    "ps": ("psum", [128, NBANKS * BANK], "float32"),
    "yb": ("sbuf", [128, N * NC], "float32"),
}
SEMAPHORES = (
    ["l_xk", "l_wk0", "l_wk1", "l_xq", "l_wq0", "q_xk", "q_xq", "a_k", "a_q", "q_k", "q_q", "st", "sent"]
    + ["q_wk%d" % i for i in range(G)] + ["q_wq%d" % i for i in range(G)]
    + ["m_k%d" % i for i in range(G)] + ["m_q%d" % i for i in range(G)]
    + ["c%d" % j for j in range(N)] + ["s%d" % j for j in range(N)]
    + ["m_y%d" % t for t in range(N)] + ["cp%d" % t for t in range(N)]
)

SPLIT_PAIRS = 2
WK_LOADS = [(0, 3), (3, 4)]

_CACHE = {}


def _bits(mask):
    return [b for b in range(16) if (mask >> b) & 1]


def _mask(bits):
    return sum(1 << b for b in bits)


def _plan(T, topo, j):
    if j in _CACHE:
        return _CACHE[j]
    cores = list(T.cores)
    R = cores[j]
    others = sorted((i for i in range(N) if i != j), key=lambda i: (i - j) % N)
    mate = [i for i in others if topo.mates(R, cores[i])]
    same = [i for i in others if topo.same_plane(R, cores[i])]
    pairs = [[s] + [i for i in others if topo.mates(cores[s], cores[i])] for s in same]
    chip = [c for c in range(WORLD) if c != R and topo.host(c) == topo.host(R) and topo.chip(c) == topo.chip(R)]
    ports = [c for c in chip if all(topo.may_write(c, cores[i]) for i in others)]
    ports.sort(key=lambda c: (topo.die(c) == topo.die(R), c))
    plain = [c for c in chip if c not in ports and all(topo.may_write(c, cores[i]) for i in same)]
    plain.sort(key=lambda c: (topo.die(c) != topo.die(R), c))
    near, far = pairs[:SPLIT_PAIRS], pairs[SPLIT_PAIRS:]
    parcels = [(R, mate + [p[1] for p in near])]
    for h, p in enumerate(far):
        parcels.append((ports[h], p))
    parcels.append((plain[0], [p[0] for p in near]))
    _CACHE[j] = parcels
    return parcels


def _codes(T, j):
    return T.kc[:, 128 * j:128 * j + 128].bitcast(dt.uint8)


def _plane(T, j):
    return T.ks[:, 128 * j:128 * j + 128]


def _transfer(T, topo, core, j, dst_cores, mask, codes):
    ids = []
    for d in dst_cores:
        rid, pid = topo.addr(d, core)
        ids.append(DstId(rid=rid, pnc=pid))
    ap = _codes(T, j) if codes else _plane(T, j)
    return RemoteDMATransfer(dst_ids=ids, dma_engine_mask=mask, remote_sem=T.sem[("c%d" if codes else "s%d") % j],
                             srcs=[ap], dsts=[ap] * len(dst_cores))


def _masks(T, topo, j):
    cores = list(T.cores)
    R = cores[j]
    parcels = _plan(T, topo, j)
    off = topo.mask(R, cores[parcels[0][1][0]])
    hs = [p[0] for p in parcels if p[0] != R]
    on = topo.mask(R, hs[0]) if hs else 0
    return _mask([b for b in _bits(on) if b not in _bits(off)]), off


def _helper(g, core, T, topo, j, dsts):
    cores = list(T.cores)
    on, _ = _masks(T, topo, j)
    m = topo.mask(core, cores[dsts[0]])
    g.wait_ge(T.sem["s%d" % j], len(_bits(on)))
    g.remote_dma_fused([_transfer(T, topo, core, j, [cores[d] for d in dsts], m, False)], local_sem=T.sem.sent)
    g.wait_ge(T.sem["c%d" % j], len(_bits(on)))
    for d in dsts:
        g.remote_dma_fused([_transfer(T, topo, core, j, [cores[d]], m, True)], local_sem=T.sem.sent)
    g.wait_ge(T.sem.sent, (1 + len(dsts)) * len(_bits(m)))


def _tile(g, T, x_t, w_t, x_c, x_s, w_c, w_s, tile, out_c, out_s, tag, bank0, loads):
    S = T.sem
    v, t, a = g.vector, g.tensor, g.scalar
    v.wait_ge(S["l_x" + tag], 16)
    v.quantize_mx(x_c[:], x_s[:], x_t[:]).then_inc(S["q_x" + tag], 1)
    t.wait_ge(S["q_x" + tag], 1)
    for n, (lo, hi) in enumerate(loads):
        v.wait_ge(S["l_w%s%d" % (tag, n)], 16)
        for i in range(lo, hi):
            v.quantize_mx(w_c[:, 128 * i:128 * i + 128], w_s[:, 128 * i:128 * i + 128],
                          w_t[:, 512 * i:512 * i + 512]).then_inc(S["q_w%s%d" % (tag, i)], 1)
            z = T.ps[:, BANK * (bank0 + i):BANK * (bank0 + i) + NC]
            t.wait_ge(S["q_w%s%d" % (tag, i)], 1)
            t.matmul_mx(z, w_c[:, 128 * i:128 * i + 128], w_s[:, 128 * i:128 * i + 128], x_c[:], x_s[:],
                        True, True).then_inc(S["m_%s%d" % (tag, i)], 1)
            a.wait_ge(S["m_%s%d" % (tag, i)], 1)
            a.activation(tile[:, i:4 * NC:4], z, ActivationFunctionType.Relu, scale=C).then_inc(S["a_" + tag], 1)
    v.wait_ge(S["a_" + tag], G)
    v.quantize_mx(out_c, out_s, tile[:]).then_inc(S["q_" + tag], 1)


def rank_program(g, core, T, topo):
    cores = list(T.cores)
    r = T.rank_of(core)
    if r is None:
        for j in range(N):
            for snd, dsts in _plan(T, topo, j):
                if snd == core:
                    _helper(g, core, T, topo, j, dsts)
        return
    S = T.sem

    (a0, b0), (a1, b1) = WK_LOADS
    g.sync.dma_start(T.xk_t[:], T.xk[:]).then_inc(S.l_xk, 16)
    g.scalar.dma_start(T.wk_t[:, 512 * a0:512 * b0], T.wk[:, 512 * a0:512 * b0]).then_inc(S.l_wk0, 16)
    g.sync.dma_start(T.wk_t[:, 512 * a1:512 * b1], T.wk[:, 512 * a1:512 * b1]).then_inc(S.l_wk1, 16)
    g.sync.dma_start(T.xq_t[:], T.xq[:]).then_inc(S.l_xq, 16)
    g.scalar.dma_start(T.wq_t[:], T.wq[:]).then_inc(S.l_wq0, 16)

    _tile(g, T, T.xk_t, T.wk_t, T.xk_c, T.xk_s, T.wk_c, T.wk_s, T.k_t,
          T.kc[:, 128 * r:128 * r + 128], T.ks[:, 128 * r:128 * r + 128], "k", 0, WK_LOADS)
    _tile(g, T, T.xq_t, T.wq_t, T.xq_c, T.xq_s, T.wq_c, T.wq_s, T.q_t, T.q_c[:], T.q_s[:], "q", G, [(0, G)])

    parcels = _plan(T, topo, r)
    on, off = _masks(T, topo, r)
    hs = [p[0] for p in parcels if p[0] != core]
    own = [cores[d] for p in parcels if p[0] == core for d in p[1]]
    g.wait_ge(S.q_k, 1)
    for dst, m in ((hs, on), (own, off)):
        g.remote_dma_fused([_transfer(T, topo, core, r, dst, m, False)], local_sem=S.sent)
        g.remote_dma_fused([_transfer(T, topo, core, r, dst, m, True)], local_sem=S.sent)
    sent = 2 * len(_bits(on)) + 2 * len(_bits(off))

    when, unit, count = {r: (0, 0)}, {r: (0, 0)}, {}
    for j in range(N):
        if j == r:
            continue
        for p, (snd, dsts) in enumerate(_plan(T, topo, j)):
            if r in dsts:
                count[j] = len(_bits(topo.mask(snd, core)))
                when[j] = (1, dsts.index(r)) if snd == cores[j] else (2 + dsts.index(r), p)
                unit[j] = (0, 0) if topo.mates(cores[j], core) else (1, j)
    seq = sorted(when, key=lambda j: when[j])
    t = g.tensor
    t.wait_ge(S.q_k, 1)
    t.wait_ge(S.q_q, 1)
    for n, j in enumerate(seq):
        if j != r:
            t.wait_ge(S["s%d" % j], count[j])
            t.wait_ge(S["c%d" % j], count[j])
        if n >= NBANKS:
            t.wait_ge(S["cp%d" % (n - NBANKS)], 1)
        z = T.ps[:, BANK * (n % NBANKS):BANK * (n % NBANKS) + NC]
        t.matmul_mx(z, T.kc[:, 128 * j:128 * j + 128], T.ks[:, 128 * j:128 * j + 128], T.q_c[:], T.q_s[:],
                    True, True).then_inc(S["m_y%d" % n], 1)
        out = T.yb[:, NC * j:NC * j + NC]
        if n % 2 == 0:
            g.scalar.wait_ge(S["m_y%d" % n], 1)
            g.scalar.activation(out, z, ActivationFunctionType.Copy).then_inc(S["cp%d" % n], 1)
        else:
            g.vector.wait_ge(S["m_y%d" % n], 1)
            g.vector.tensor_copy(out, z).then_inc(S["cp%d" % n], 1)

    units = {}
    for j in seq:
        units.setdefault(unit[j], []).append(j)
    stores = 0
    for js in sorted(units.values(), key=lambda js: max(seq.index(j) for j in js)):
        js = sorted(js)
        for j in js:
            g.sync.wait_ge(S["cp%d" % seq.index(j)], 1)
        runs = []
        for j in js:
            if runs and runs[-1][1] == j:
                runs[-1][1] = j + 1
            else:
                runs.append([j, j + 1])
        for a, b in runs:
            g.sync.dma_start(T.y[:, NC * a:NC * b], T.yb[:, NC * a:NC * b]).then_inc(S.st, 16)
            stores += 1
    g.sync.wait_ge(S.st, 16 * stores)
    g.wait_ge(S.sent, sent)
